import numpy as np
import ml_dtypes


def mxq(x, axis, fmt="e4m3"):
    dtype, down = {"e4m3": (ml_dtypes.float8_e4m3fn, 7), "e5m2": (ml_dtypes.float8_e5m2, 14)}[fmt]
    v = np.moveaxis(np.asarray(x, np.float32).astype(ml_dtypes.bfloat16).astype(np.float64), axis, -1)
    blocks = v.reshape(v.shape[:-1] + (-1, 32))
    amax = np.abs(blocks).max(-1, keepdims=True)
    byte = np.maximum(np.where(amax > 0, np.frexp(amax)[1] - 1 + 127, 0) - down, 1)
    scale = np.exp2(byte - 127.0)
    codes = (blocks / scale).astype(np.float32).astype(dtype).astype(np.float64)
    return np.moveaxis((codes * scale).reshape(v.shape), -1, axis)


WIDE = False


def mx_kscale(k):
    if not WIDE:
        return np.ones(k)
    levels = np.array([10, -10, 5, -5, 0])
    if k % 512:
        return np.exp2(np.random.permutation(np.resize(levels, k // 32))).repeat(32)
    a = np.empty((k // 512, 16))
    for p in range(k // 512):
        a[p, :8] = np.random.permutation(np.resize(levels, 8))
        for g in range(8):
            far = levels[np.abs(levels - a[p, g]) >= 10]
            a[p, g + 8] = far[np.random.randint(len(far))]
    return np.exp2(a.ravel()).repeat(32)


def f64(x):
    return np.asarray(x).astype(np.float64)


def striped(idx):
    return np.tile(idx.reshape(-1, 16).T, (8, 1)).astype(np.uint16)


def unstriped(offs):
    return offs[:16].T.reshape(-1).astype(np.int64)


def striped8(idx):
    return np.concatenate([x.reshape(-1, 16).T for x in idx]).astype(np.uint16)


def runs(offs, k):
    lists = np.stack([offs[16 * r : 16 * r + 16].T.reshape(-1) for r in range(8)]).astype(np.int64)
    return lists[np.arange(k) % 512 // 64]


def pack_weight(w):
    k, n = w.shape
    w = f64(np.asarray(w, np.float32).astype(ml_dtypes.bfloat16)).reshape(k // 32, 32, n)
    amax = np.abs(w).max(1)
    byte = np.clip(np.where(amax > 0, np.frexp(amax)[1] - 1 + 127 - 7, 1), 1, 254)
    scaled = (w * np.exp2(127.0 - byte)[:, None, :]).reshape(k, n).astype(np.float32)
    words = np.ascontiguousarray(scaled.reshape(k // 512, 128, 4, n).transpose(0, 1, 3, 2)).astype(ml_dtypes.float8_e4m3fn).view(np.uint8)
    return words, np.ascontiguousarray(byte.astype(np.uint8).reshape(k // 512, 16, n))


def unpack_weight(words, scales):
    g, p, n, _ = words.shape
    vals = np.ascontiguousarray(words).view(ml_dtypes.float8_e4m3fn).astype(np.float64) * np.repeat(np.exp2(scales.astype(np.float64) - 127.0), 8, axis=1)[..., None]
    return vals.transpose(0, 1, 3, 2).reshape(g * 512, n)


def relu(v):
    return np.maximum(v, 0.0)


K, T, S, N, H, J, G, U = 512, 1024, 512, 512, 512, 512, 2048, 1024


def setup_inputs():
    n = np.random.standard_normal
    s = mx_kscale(K)[:, None]
    u = mx_kscale(S)
    packed_xT = pack_weight(n((K, T)) * s)
    packed_dT = pack_weight(n((K, G)) / s)
    return {
        "x_words": packed_xT[0],
        "x_scales": packed_xT[1],
        "w1": (n((K, H)) / np.sqrt(K) / s).astype(np.float32),
        "tab": n((H, J)).astype(np.float32),
        "gs": (np.random.uniform(0.5, 1.5, (K, 1)) * s).astype(np.float32),
        "d_words": packed_dT[0],
        "d_scales": packed_dT[1],
        "res": (1.5 * n((N, U))).astype(np.float32),
        "gn": (np.random.uniform(0.5, 1.5, (H, 1)) * u[:, None]).astype(np.float32),
        "w2": (n((H, N)) / np.sqrt(H) / u[:, None]).astype(np.float32),
        "offs": striped(np.random.permutation(T)[:S]),
        "n1": striped8(np.random.randint(0, J, (8, S))),
        "n2": striped8(np.random.randint(0, J, (8, S))),
        "n3": striped8(np.stack([np.random.permutation(S) for _ in range(8)])),
        "kidx": striped8(np.random.randint(0, G, (8, H))),
        "n4": striped8(np.stack([np.random.permutation(U)[:S] for _ in range(8)])),
        "n5": striped8(np.stack([np.random.permutation(S) for _ in range(8)])),
    }


def reference(x_words, x_scales, w1, tab, gs, d_words, d_scales, res, gn, w2, offs, n1, n2, n3, kidx, n4, n5):
    d_kidx = unpack_weight(d_words, d_scales)[np.arange(K)[:, None], runs(kidx, K)]
    xq = unpack_weight(x_words, x_scales)[:, unstriped(offs)]
    y = mxq(f64(w1), 0, "e4m3").T @ xq
    z = f64(gs) * ((y[np.arange(H)[:, None], runs(n3, H)]) * (f64(tab)[np.arange(H)[:, None], runs(n1, H)]) + f64(tab)[np.arange(H)[:, None], runs(n2, H)])
    s = 0.0625 * ((d_kidx.T @ mxq(z, 0, "e4m3")))
    nw = s - (relu(s[np.arange(H)[:, None], runs(n5, H)]))
    pg = np.zeros((H, U))
    pg[np.arange(H)[:, None], runs(n4, H)] = nw
    z2 = f64(gn) * pg
    return f64(res) + (mxq(f64(w2), 0, "e4m3").T @ mxq(z2, 0, "e4m3"))

@@ -1,0 +1,242 @@
+from contextlib import ExitStack
+
+import concourse.mybir as mybir
+
+F32 = mybir.dt.float32
+BF16 = mybir.dt.bfloat16
+I32 = mybir.dt.int32
+U32 = mybir.dt.uint32
+U16 = mybir.dt.uint16
+U8 = mybir.dt.uint8
+FP8X4 = mybir.dt.float8_e4m3fn_x4
+ALU = mybir.AluOpType
+ACT = mybir.ActivationFunctionType
+
+P = 128
+R = 4
+K, T, S, N, H, J, G, U = 512, 1024, 512, 512, 512, 512, 2048, 1024
+FLOPS = 2 * K * H * S + 2 * K * H * S + 2 * H * N * U
+Z_SLICES = (256, 128, 128)
+OUT_CHUNKS = (128, 128, 256, 256, 256)
+
+
+def tile_picked_pqkkindapagez_none_p_kernel(tc, x_words, x_scales, w1, tab, gs, d_words, d_scales, res, gn, w2, offs, n1, n2, n3, kidx, n4, n5, out):
+    nc = tc.nc
+    with ExitStack() as ctx:
+        keep = ctx.enter_context(tc.tile_pool(name="keep", bufs=1))
+        psum = ctx.enter_context(tc.psum_pool(name="psum", bufs=1))
+
+        def sb(name, shape, dtype, tag=None):
+            return keep.tile(shape, dtype, name=name, tag=tag or name, align_bytes=64)
+
+        def load_list(name, src):
+            t = keep.tile([P, S // 16], U16, name=name)
+            nc.sync.dma_start(t[:], src)
+            return t
+
+        x_sc = sb("x_sc", [P, T], U8)
+        d_sc = sb("d_sc", [P, G], U8)
+        key_sc = sb("key_sc", [P, H], U8)
+        nc.vector.memset(x_sc[:].bitcast(I32), 0)
+        nc.vector.memset(d_sc[:].bitcast(I32), 0)
+        nc.vector.memset(key_sc[:].bitcast(I32), 0)
+        page = [sb("page%d" % t, [P, U], F32) for t in range(R)]
+        for t in range(2):
+            nc.vector.memset(page[t][:], 0.0)
+        zero = sb("zero", [P, 8], F32)
+        nc.gpsimd.memset(zero[:], 0.0)
+        for t in range(2, R):
+            nc.scalar.copy(page[t][:], zero[:, 0:1].to_broadcast([P, U]))
+
+        tab_v = tab.rearrange("(p t) c -> t p c", t=R)
+        tab_sb = [sb("tab%d" % t, [P, J], F32) for t in range(R)]
+        l_n1 = load_list("l_n1", n1)
+        nc.sync.dma_start(tab_sb[0][:], tab_v[0])
+        l_offs = load_list("l_offs", offs)
+        x_w = sb("x_w", [P, T], U32)
+        nc.sync.dma_start(x_w[:].bitcast(I32), x_words[0].rearrange("p n r -> p (n r)").bitcast(I32))
+        nc.sync.dma_start(tab_sb[1][:], tab_v[1])
+        w1_v = w1.rearrange("(p j) c -> p j c", j=R)
+        w1_raw = [sb("w1_raw%d" % h, [P, R, H // 2], F32) for h in range(2)]
+        nc.sync.dma_start(w1_raw[0][:], w1_v[:, :, 0 : H // 2])
+        nc.sync.dma_start(tab_sb[2][:], tab_v[2])
+        nc.sync.dma_start(w1_raw[1][:], w1_v[:, :, H // 2 : H])
+        xs_v = x_scales[0].bitcast(I32).rearrange("(q j) c -> j q c", j=4)
+        for j in range(4):
+            nc.sync.dma_start(x_sc[j:P:32, :].bitcast(I32), xs_v[j])
+        gs_sb = sb("gs_sb", [P, R], F32)
+        nc.sync.dma_start(gs_sb[:], gs.rearrange("(p t) o -> p (t o)", t=R))
+        nc.sync.dma_start(tab_sb[3][:], tab_v[3])
+        l_kidx = load_list("l_kidx", kidx)
+        ds_v = d_scales[0].bitcast(I32).rearrange("(r e) c -> e r c", e=2)
+        for e in range(2):
+            nc.sync.dma_start(d_sc[e:P:16, :].bitcast(I32), ds_v[e])
+        d_w = sb("d_w", [P, G], U32)
+        nc.sync.dma_start(d_w[:].bitcast(I32), d_words[0].rearrange("p n r -> p (n r)").bitcast(I32))
+        l_n3 = load_list("l_n3", n3)
+        l_n2 = load_list("l_n2", n2)
+        gn_sb = sb("gn_sb", [P, R], F32)
+        nc.sync.dma_start(gn_sb[:], gn.rearrange("(p t) o -> p (t o)", t=R))
+        w2_raw = sb("w2_raw", [P, R, N], F32)
+        nc.sync.dma_start(w2_raw[:], w2.rearrange("(p j) c -> p j c", j=R))
+        l_n5 = load_list("l_n5", n5)
+        l_n4 = load_list("l_n4", n4)
+        res_v = res.rearrange("(t p) w -> p t w", p=P)
+        out_v = out.rearrange("(t p) w -> p t w", p=P)
+        starts = [sum(OUT_CHUNKS[:c]) for c in range(len(OUT_CHUNKS))]
+        res_sb = {}
+        for c, width in enumerate(OUT_CHUNKS):
+            per = 512 // width
+            for u in range(R // per):
+                res_sb[(c, u)] = sb("res%d_%d" % (c, u), [P, per, width], F32)
+                nc.sync.dma_start(res_sb[(c, u)][:], res_v[:, per * u : per * (u + 1), starts[c] : starts[c] + width])
+
+        kind1 = [sb("kind1_%d" % t, [P, S], F32) for t in range(R)]
+
+        def gather_n1(t):
+            for h in range(2):
+                nc.vector.tensor_copy(kind1[t][:, 256 * h : 256 * h + 256], tab_sb[t][:].indirect(l_n1[:, 16 * h : 16 * h + 16]))
+
+        gather_n1(0)
+        tok_w = sb("tok_w", [P, S], U32)
+        nc.vector.tensor_copy(tok_w[:], x_w[:].indirect(l_offs[:]))
+        gather_n1(1)
+        gather_n1(2)
+        tok_sc = sb("tok_sc", [P, S], U8)
+        nc.vector.tensor_copy(tok_sc[:], x_sc[:].indirect(l_offs[:]))
+
+        w1_bf = sb("w1_bf", [P, R, P, R], BF16)
+        for h in range(2):
+            nc.scalar.copy(w1_bf[:, :, 64 * h : 64 * h + 64, :].rearrange("p t m j -> p m t j"), w1_raw[h][:].rearrange("p j (m t) -> p m t j", t=R))
+        w1_w = sb("w1_w", [P, H], U32)
+        w1_sc = sb("w1_sc", [P, H], U8)
+        nc.vector.quantize_mx(w1_w[:].bitcast(FP8X4), w1_sc[:], w1_bf[:].rearrange("p t m j -> p (t m j)"))
+        gather_n1(3)
+
+        y_sb = [sb("y%d" % t, [P, S], F32) for t in range(R)]
+        tabg = [sb("tabg%d" % t, [P, J], F32) for t in range(R)]
+        for t in range(R):
+            bank = psum.tile([P, S], F32, name="y_bank%d" % t, tag="a%d" % t)
+            cols = slice(P * t, P * t + P)
+            nc.tensor.matmul_mx(bank[:], lhsT=w1_w[:, cols].bitcast(FP8X4), lhsT_scale=w1_sc[:, cols], rhs=tok_w[:].bitcast(FP8X4), rhs_scale=tok_sc[:], start=True, stop=True)
+            nc.scalar.activation(y_sb[t][:], bank[:], ACT.Copy, scale=gs_sb[:, t : t + 1])
+            nc.scalar.activation(tabg[t][:], tab_sb[t][:], ACT.Copy, scale=gs_sb[:, t : t + 1])
+
+        pick_sc = sb("pick_sc", [P, H], U8)
+        nc.vector.tensor_copy(pick_sc[:], d_sc[:].indirect(l_kidx[:]))
+        pick_w = sb("pick_w", [P, H], U32)
+        nc.vector.tensor_copy(pick_w[:], d_w[:].indirect(l_kidx[:]))
+        dealt_sc = sb("dealt_sc", [P, H], U8)
+        nc.vector.tensor_copy(dealt_sc[:].rearrange("p (t b i) -> p b t i", t=R, i=16), pick_sc[:].rearrange("p (b i t) -> p b t i", t=R, i=16))
+        key_w = sb("key_w", [P, H], U32)
+        nc.vector.tensor_copy(key_w[:].rearrange("p (t b i) -> p b t i", t=R, i=4), pick_w[:].rearrange("p (b i t) -> p b t i", t=R, i=4))
+        for j in range(4):
+            src = 16 * (j // 2) + j % 2
+            nc.sync.dma_start(key_sc[j:P:32, :].bitcast(I32), dealt_sc[src:P:32, :].bitcast(I32))
+
+        gn16 = sb("gn16", [P, R], F32)
+        gn16n = sb("gn16n", [P, R], F32)
+        nc.scalar.activation(gn16[:], gn_sb[:], ACT.Copy, scale=0.0625)
+        nc.scalar.activation(gn16n[:], gn_sb[:], ACT.Copy, scale=-0.0625)
+
+        w2_bf = sb("w2_bf", [P, N, R], BF16)
+        nc.scalar.copy(w2_bf[:].rearrange("p (c i) j -> p c j i", i=4), w2_raw[:].rearrange("p j (c i) -> p c j i", i=4))
+
+        score = [sb("score%d" % t, [P, 2 * S], F32) for t in range(R)]
+        s_bank = [psum.tile([P, S], F32, name="s_bank%d" % t, tag="b%d" % t) for t in range(R)]
+        c0 = 0
+        for i, width in enumerate(Z_SLICES):
+            last = i == len(Z_SLICES) - 1
+            cols = slice(c0, c0 + width)
+            lcols = slice(c0 // 16, (c0 + width) // 16)
+            prod = sb("prod%d" % i, [P, R, width], F32)
+            z32 = sb("z32_%d" % i, [P, R, width], F32)
+            for step in range(R + 1):
+                if step < R:
+                    nc.vector.tensor_tensor(prod[:, step, :], y_sb[step][:].indirect(l_n3[:, lcols]), kind1[step][:, cols], ALU.mult)
+                if step > 0:
+                    nc.vector.tensor_tensor(z32[:, step - 1, :], tabg[step - 1][:].indirect(l_n2[:, lcols]), prod[:, step - 1, :], ALU.add)
+            z_bf = sb("z_bf%d" % i, [P, width, R], BF16)
+            dst = z_bf[:].rearrange("p (c i) j -> p c j i", i=4)
+            srcv = z32[:].rearrange("p j (c i) -> p c j i", i=4)
+            if last:
+                nc.vector.tensor_copy(dst, srcv)
+            else:
+                nc.scalar.copy(dst, srcv)
+            z_w = sb("z_w%d" % i, [P, width], U32)
+            z_sc = sb("z_sc%d" % i, [P, width], U8)
+            nc.vector.quantize_mx(z_w[:].bitcast(FP8X4), z_sc[:], z_bf[:].rearrange("p c j -> p (c j)"))
+            pos = sb("pos%d" % i, [P, R, width], F32)
+            for t in range(R):
+                kc = slice(P * t, P * t + P)
+                nc.tensor.matmul_mx(s_bank[t][:, cols], lhsT=key_w[:, kc].bitcast(FP8X4), lhsT_scale=key_sc[:, kc], rhs=z_w[:].bitcast(FP8X4), rhs_scale=z_sc[:], start=True, stop=True)
+            for t in range(R):
+                if last and t == 0:
+                    nc.vector.tensor_scalar(score[t][:, cols], s_bank[t][:, cols], 0.0, gn16n[:, t : t + 1], ALU.max, ALU.mult)
+                else:
+                    nc.scalar.activation(pos[:, t, :], s_bank[t][:, cols], ACT.Relu)
+                    nc.scalar.activation(score[t][:, cols], pos[:, t, :], ACT.Copy, scale=gn16n[:, t : t + 1])
+                nc.scalar.activation(score[t][:, S + c0 : S + c0 + width], s_bank[t][:, cols], ACT.Copy, scale=gn16[:, t : t + 1])
+            c0 = c0 + width
+
+        def quantize_w2(h, tag):
+            words = sb("w2_w%d" % h, [P, N // 2], U32, tag=tag)
+            scales = sb("w2_sc%d" % h, [P, N // 2], U8)
+            nc.vector.quantize_mx(words[:].bitcast(FP8X4), scales[:], w2_bf[:, 256 * h : 256 * h + 256, :].rearrange("p c j -> p (c j)"))
+            return words, scales
+
+        w2_q = [quantize_w2(0, "z32_%d" % (len(Z_SLICES) - 1))]
+
+        z2_bf = [sb("z2_bf%d" % c, [P, width, R], BF16) for c, width in enumerate(OUT_CHUNKS)]
+
+        def weave(t, c):
+            nc.scalar.copy(z2_bf[c][:, :, t], page[t][:, starts[c] : starts[c] + OUT_CHUNKS[c]])
+
+        fetched = []
+
+        def fetch(t, tag):
+            fetched.append(sb("fetched%d" % t, [P, S], F32, tag=tag))
+            nc.vector.tensor_copy(fetched[t][:], score[t][:].indirect(l_n5[:]))
+
+        def put(t):
+            nc.vector.tensor_tensor(page[t][:].indirect(l_n4[:]), fetched[t][:], score[t][:, S : 2 * S], ALU.add)
+            for c in range(len(OUT_CHUNKS)):
+                weave(t, c)
+
+        fetch(0, "fa")
+        fetch(1, "fb")
+        put(0)
+        fetch(2, "fa")
+        put(1)
+        put(2)
+        fetch(3, "fa")
+        w2_q.append(quantize_w2(1, "score2"))
+        put(3)
+
+        z2_q = []
+
+        def quantize_z2(c):
+            width = OUT_CHUNKS[c]
+            words = sb("z2_w%d" % c, [P, width], U32, tag=("res%d_0" % (c - 2) if c >= 2 else None))
+            scales = sb("z2_sc%d" % c, [P, width], U8)
+            nc.vector.quantize_mx(words[:].bitcast(FP8X4), scales[:], z2_bf[c][:].rearrange("p c j -> p (c j)"))
+            z2_q.append((words, scales))
+
+        quantize_z2(0)
+        nb = 0
+        for c, width in enumerate(OUT_CHUNKS):
+            if c + 1 < len(OUT_CHUNKS):
+                quantize_z2(c + 1)
+            cols = slice(starts[c], starts[c] + width)
+            per = 512 // width
+            for u in range(R // per):
+                bank = psum.tile([P, per, width], F32, name="o_bank%d_%d" % (c, u), tag="%s%d" % ("ab"[nb // 4], nb % 4))
+                nb = nb + 1
+                for v in range(per):
+                    m = per * u + v
+                    ww, ws = w2_q[m // 2]
+                    mc = slice(P * (m % 2), P * (m % 2 + 1))
+                    nc.tensor.matmul_mx(bank[:, v, :], lhsT=ww[:, mc].bitcast(FP8X4), lhsT_scale=ws[:, mc], rhs=z2_q[c][0][:].bitcast(FP8X4), rhs_scale=z2_q[c][1][:], start=True, stop=True)
+                o_sb = sb("o_sb%d_%d" % (c, u), [P, per, width], F32)
+                nc.vector.tensor_tensor(o_sb[:], bank[:], res_sb[(c, u)][:], ALU.add)
+                nc.sync.dma_start(out_v[:, per * u : per * (u + 1), cols], o_sb[:])

@@ -49,24 +49,22 @@ def tile_picked_pqkkindapagez_none_p_kernel(tc, x_words, x_scales, w1, tab, gs, 
             nc.scalar.copy(page[t][:], zero[:, 0:1].to_broadcast([P, U]))
 
         tab_v = tab.rearrange("(p t) c -> t p c", t=R)
-        tab_sb = [sb("tab%d" % t, [P, J], F32) for t in range(R)]
+        tab_sb = [sb("tab%d" % t, [P, 2 * J], F32) for t in range(R)]
+        nc.sync.dma_start(tab_sb[0][:, 0:J], tab_v[0])
         l_n1 = load_list("l_n1", n1)
-        nc.sync.dma_start(tab_sb[0][:], tab_v[0])
         l_offs = load_list("l_offs", offs)
         x_w = sb("x_w", [P, T], U32)
         nc.sync.dma_start(x_w[:].bitcast(I32), x_words[0].rearrange("p n r -> p (n r)").bitcast(I32))
-        nc.sync.dma_start(tab_sb[1][:], tab_v[1])
-        w1_v = w1.rearrange("(p j) c -> p j c", j=R)
-        w1_raw = [sb("w1_raw%d" % h, [P, R, H // 2], F32) for h in range(2)]
-        nc.sync.dma_start(w1_raw[0][:], w1_v[:, :, 0 : H // 2])
-        nc.sync.dma_start(tab_sb[2][:], tab_v[2])
-        nc.sync.dma_start(w1_raw[1][:], w1_v[:, :, H // 2 : H])
+        nc.sync.dma_start(tab_sb[1][:, 0:J], tab_v[1])
+        w1_raw = sb("w1_raw", [P, R, H], F32)
+        nc.sync.dma_start(w1_raw[:], w1.rearrange("(p j) c -> p j c", j=R))
+        nc.sync.dma_start(tab_sb[2][:, 0:J], tab_v[2])
+        nc.sync.dma_start(tab_sb[3][:, 0:J], tab_v[3])
         xs_v = x_scales[0].bitcast(I32).rearrange("(q j) c -> j q c", j=4)
         for j in range(4):
             nc.sync.dma_start(x_sc[j:P:32, :].bitcast(I32), xs_v[j])
         gs_sb = sb("gs_sb", [P, R], F32)
         nc.sync.dma_start(gs_sb[:], gs.rearrange("(p t) o -> p (t o)", t=R))
-        nc.sync.dma_start(tab_sb[3][:], tab_v[3])
         l_kidx = load_list("l_kidx", kidx)
         ds_v = d_scales[0].bitcast(I32).rearrange("(r e) c -> e r c", e=2)
         for e in range(2):
@@ -92,35 +90,33 @@ def tile_picked_pqkkindapagez_none_p_kernel(tc, x_words, x_scales, w1, tab, gs, 
                 nc.sync.dma_start(res_sb[(c, u)][:], res_v[:, per * u : per * (u + 1), starts[c] : starts[c] + width])
 
         kind1 = [sb("kind1_%d" % t, [P, S], F32) for t in range(R)]
+        tabg = [sb("tabg%d" % t, [P, J], F32) for t in range(R)]
 
-        def gather_n1(t):
-            for h in range(2):
-                nc.vector.tensor_copy(kind1[t][:, 256 * h : 256 * h + 256], tab_sb[t][:].indirect(l_n1[:, 16 * h : 16 * h + 16]))
+        def gather_kinds(t):
+            nc.vector.tensor_copy(kind1[t][:], tab_sb[t][:].indirect(l_n1[:]))
 
-        gather_n1(0)
+        gather_kinds(0)
         tok_w = sb("tok_w", [P, S], U32)
         nc.vector.tensor_copy(tok_w[:], x_w[:].indirect(l_offs[:]))
-        gather_n1(1)
-        gather_n1(2)
+        gather_kinds(1)
         tok_sc = sb("tok_sc", [P, S], U8)
         nc.vector.tensor_copy(tok_sc[:], x_sc[:].indirect(l_offs[:]))
 
         w1_bf = sb("w1_bf", [P, R, P, R], BF16)
-        for h in range(2):
-            nc.scalar.copy(w1_bf[:, :, 64 * h : 64 * h + 64, :].rearrange("p t m j -> p m t j"), w1_raw[h][:].rearrange("p j (m t) -> p m t j", t=R))
+        nc.scalar.copy(w1_bf[:].rearrange("p t m j -> p m t j"), w1_raw[:].rearrange("p j (m t) -> p m t j", t=R))
         w1_w = sb("w1_w", [P, H], U32)
         w1_sc = sb("w1_sc", [P, H], U8)
         nc.vector.quantize_mx(w1_w[:].bitcast(FP8X4), w1_sc[:], w1_bf[:].rearrange("p t m j -> p (t m j)"))
-        gather_n1(3)
+        gather_kinds(2)
+        gather_kinds(3)
 
         y_sb = [sb("y%d" % t, [P, S], F32) for t in range(R)]
-        tabg = [sb("tabg%d" % t, [P, J], F32) for t in range(R)]
         for t in range(R):
             bank = psum.tile([P, S], F32, name="y_bank%d" % t, tag="a%d" % t)
             cols = slice(P * t, P * t + P)
             nc.tensor.matmul_mx(bank[:], lhsT=w1_w[:, cols].bitcast(FP8X4), lhsT_scale=w1_sc[:, cols], rhs=tok_w[:].bitcast(FP8X4), rhs_scale=tok_sc[:], start=True, stop=True)
-            nc.scalar.activation(y_sb[t][:], bank[:], ACT.Copy, scale=gs_sb[:, t : t + 1])
-            nc.scalar.activation(tabg[t][:], tab_sb[t][:], ACT.Copy, scale=gs_sb[:, t : t + 1])
+            nc.scalar.activation(y_sb[t][:, 0:S], bank[:], ACT.Copy, scale=gs_sb[:, t : t + 1])
+            nc.scalar.activation(tabg[t][:, 0:J], tab_sb[t][:, 0:J], ACT.Copy, scale=gs_sb[:, t : t + 1])
 
         pick_sc = sb("pick_sc", [P, H], U8)
         nc.vector.tensor_copy(pick_sc[:], d_sc[:].indirect(l_kidx[:]))
@@ -143,13 +139,25 @@ def tile_picked_pqkkindapagez_none_p_kernel(tc, x_words, x_scales, w1, tab, gs, 
         nc.scalar.copy(w2_bf[:].rearrange("p (c i) j -> p c j i", i=4), w2_raw[:].rearrange("p j (c i) -> p c j i", i=4))
 
         score = [sb("score%d" % t, [P, 2 * S], F32) for t in range(R)]
+        own = [sb("own%d" % t, [P, S], F32) for t in range(R)]
         s_bank = [psum.tile([P, S], F32, name="s_bank%d" % t, tag="b%d" % t) for t in range(R)]
+        pos = [sb("pos%d" % t, [P, S], F32) for t in range(R)]
+
+        def negative_part(t, cols):
+            nc.scalar.activation(pos[t][:, cols], s_bank[t][:, cols], ACT.Relu)
+            nc.scalar.activation(score[t][:, cols], pos[t][:, cols], ACT.Copy, scale=gn16n[:, t : t + 1])
+
+        def own_part(t, cols):
+            nc.scalar.activation(own[t][:, cols], s_bank[t][:, cols], ACT.Copy, scale=gn16[:, t : t + 1])
+
         c0 = 0
+        first = slice(0, Z_SLICES[0])
+        rest = slice(Z_SLICES[0], S)
         for i, width in enumerate(Z_SLICES):
             last = i == len(Z_SLICES) - 1
             cols = slice(c0, c0 + width)
             lcols = slice(c0 // 16, (c0 + width) // 16)
-            prod = sb("prod%d" % i, [P, R, width], F32)
+            prod = sb("prod%d" % i, [P, R, width], F32, tag=("z_bf0" if last else None))
             z32 = sb("z32_%d" % i, [P, R, width], F32)
             for step in range(R + 1):
                 if step < R:
@@ -166,52 +174,54 @@ def tile_picked_pqkkindapagez_none_p_kernel(tc, x_words, x_scales, w1, tab, gs, 
             z_w = sb("z_w%d" % i, [P, width], U32)
             z_sc = sb("z_sc%d" % i, [P, width], U8)
             nc.vector.quantize_mx(z_w[:].bitcast(FP8X4), z_sc[:], z_bf[:].rearrange("p c j -> p (c j)"))
-            pos = sb("pos%d" % i, [P, R, width], F32)
             for t in range(R):
                 kc = slice(P * t, P * t + P)
                 nc.tensor.matmul_mx(s_bank[t][:, cols], lhsT=key_w[:, kc].bitcast(FP8X4), lhsT_scale=key_sc[:, kc], rhs=z_w[:].bitcast(FP8X4), rhs_scale=z_sc[:], start=True, stop=True)
-            for t in range(R):
-                if last and t == 0:
-                    nc.vector.tensor_scalar(score[t][:, cols], s_bank[t][:, cols], 0.0, gn16n[:, t : t + 1], ALU.max, ALU.mult)
-                else:
-                    nc.scalar.activation(pos[:, t, :], s_bank[t][:, cols], ACT.Relu)
-                    nc.scalar.activation(score[t][:, cols], pos[:, t, :], ACT.Copy, scale=gn16n[:, t : t + 1])
-                nc.scalar.activation(score[t][:, S + c0 : S + c0 + width], s_bank[t][:, cols], ACT.Copy, scale=gn16[:, t : t + 1])
+            if i == 0:
+                negative_part(0, first)
+                negative_part(1, first)
+                own_part(0, first)
+                own_part(1, first)
             c0 = c0 + width
+        nc.vector.tensor_scalar(score[0][:, rest], s_bank[0][:, rest], 0.0, gn16n[:, 0:1], ALU.max, ALU.mult)
+        own_part(0, rest)
+        negative_part(1, rest)
+        own_part(1, rest)
+        for t in range(2, R):
+            negative_part(t, slice(0, S))
+            own_part(t, slice(0, S))
 
-        def quantize_w2(h, tag):
-            words = sb("w2_w%d" % h, [P, N // 2], U32, tag=tag)
-            scales = sb("w2_sc%d" % h, [P, N // 2], U8)
-            nc.vector.quantize_mx(words[:].bitcast(FP8X4), scales[:], w2_bf[:, 256 * h : 256 * h + 256, :].rearrange("p c j -> p (c j)"))
-            return words, scales
+        def quantize_w2(m0, width, tag):
+            words = sb("w2_w%d" % m0, [P, width], U32, tag=tag)
+            scales = sb("w2_sc%d" % m0, [P, width], U8)
+            nc.vector.quantize_mx(words[:].bitcast(FP8X4), scales[:], w2_bf[:, m0 : m0 + width, :].rearrange("p c j -> p (c j)"))
+            return [(words[:, b : b + P], scales[:, b : b + P]) for b in range(0, width, P)]
 
-        w2_q = [quantize_w2(0, "z32_%d" % (len(Z_SLICES) - 1))]
+        w2_q = quantize_w2(0, 2 * P, "z32_2")
 
         z2_bf = [sb("z2_bf%d" % c, [P, width, R], BF16) for c, width in enumerate(OUT_CHUNKS)]
 
         def weave(t, c):
             nc.scalar.copy(z2_bf[c][:, :, t], page[t][:, starts[c] : starts[c] + OUT_CHUNKS[c]])
 
-        fetched = []
+        fetched = [sb("fetched%d" % t, [P, S], F32) for t in range(R)]
 
-        def fetch(t, tag):
-            fetched.append(sb("fetched%d" % t, [P, S], F32, tag=tag))
-            nc.vector.tensor_copy(fetched[t][:], score[t][:].indirect(l_n5[:]))
+        def fetch(t):
+            nc.vector.tensor_tensor(fetched[t][:], score[t][:].indirect(l_n5[:]), own[t][:], ALU.add)
 
         def put(t):
-            nc.vector.tensor_tensor(page[t][:].indirect(l_n4[:]), fetched[t][:], score[t][:, S : 2 * S], ALU.add)
+            nc.vector.tensor_copy(page[t][:].indirect(l_n4[:]), fetched[t][:])
             for c in range(len(OUT_CHUNKS)):
                 weave(t, c)
 
-        fetch(0, "fa")
-        fetch(1, "fb")
+        fetch(0)
+        fetch(1)
         put(0)
-        fetch(2, "fa")
         put(1)
-        put(2)
-        fetch(3, "fa")
-        w2_q.append(quantize_w2(1, "score2"))
-        put(3)
+        for t in range(2, R):
+            fetch(t)
+            w2_q.extend(quantize_w2(P * t, P, "pos%d" % t))
+            put(t)
 
         z2_q = []
 
@@ -234,9 +244,8 @@ def tile_picked_pqkkindapagez_none_p_kernel(tc, x_words, x_scales, w1, tab, gs, 
                 nb = nb + 1
                 for v in range(per):
                     m = per * u + v
-                    ww, ws = w2_q[m // 2]
-                    mc = slice(P * (m % 2), P * (m % 2 + 1))
-                    nc.tensor.matmul_mx(bank[:, v, :], lhsT=ww[:, mc].bitcast(FP8X4), lhsT_scale=ws[:, mc], rhs=z2_q[c][0][:].bitcast(FP8X4), rhs_scale=z2_q[c][1][:], start=True, stop=True)
+                    ww, ws = w2_q[m]
+                    nc.tensor.matmul_mx(bank[:, v, :], lhsT=ww.bitcast(FP8X4), lhsT_scale=ws, rhs=z2_q[c][0][:].bitcast(FP8X4), rhs_scale=z2_q[c][1][:], start=True, stop=True)
                 o_sb = sb("o_sb%d_%d" % (c, u), [P, per, width], F32)
                 nc.vector.tensor_tensor(o_sb[:], bank[:], res_sb[(c, u)][:], ALU.add)
                 nc.sync.dma_start(out_v[:, per * u : per * (u + 1), cols], o_sb[:])

@@ -63,14 +63,14 @@ def tile_picked_pqkkindapagez_none_p_kernel(tc, x_words, x_scales, w1, tab, gs, 
         xs_v = x_scales[0].bitcast(I32).rearrange("(q j) c -> j q c", j=4)
         for j in range(4):
             nc.sync.dma_start(x_sc[j:P:32, :].bitcast(I32), xs_v[j])
+        l_kidx = load_list("l_kidx", kidx)
+        d_w = sb("d_w", [P, G], U32)
+        nc.sync.dma_start(d_w[:].bitcast(I32), d_words[0].rearrange("p n r -> p (n r)").bitcast(I32))
         gs_sb = sb("gs_sb", [P, R], F32)
         nc.sync.dma_start(gs_sb[:], gs.rearrange("(p t) o -> p (t o)", t=R))
-        l_kidx = load_list("l_kidx", kidx)
         ds_v = d_scales[0].bitcast(I32).rearrange("(r e) c -> e r c", e=2)
         for e in range(2):
             nc.sync.dma_start(d_sc[e:P:16, :].bitcast(I32), ds_v[e])
-        d_w = sb("d_w", [P, G], U32)
-        nc.sync.dma_start(d_w[:].bitcast(I32), d_words[0].rearrange("p n r -> p (n r)").bitcast(I32))
         l_n3 = load_list("l_n3", n3)
         l_n2 = load_list("l_n2", n2)
         gn_sb = sb("gn_sb", [P, R], F32)
@@ -118,10 +118,10 @@ def tile_picked_pqkkindapagez_none_p_kernel(tc, x_words, x_scales, w1, tab, gs, 
             nc.scalar.activation(y_sb[t][:, 0:S], bank[:], ACT.Copy, scale=gs_sb[:, t : t + 1])
             nc.scalar.activation(tabg[t][:, 0:J], tab_sb[t][:, 0:J], ACT.Copy, scale=gs_sb[:, t : t + 1])
 
-        pick_sc = sb("pick_sc", [P, H], U8)
-        nc.vector.tensor_copy(pick_sc[:], d_sc[:].indirect(l_kidx[:]))
         pick_w = sb("pick_w", [P, H], U32)
         nc.vector.tensor_copy(pick_w[:], d_w[:].indirect(l_kidx[:]))
+        pick_sc = sb("pick_sc", [P, H], U8)
+        nc.vector.tensor_copy(pick_sc[:], d_sc[:].indirect(l_kidx[:]))
         dealt_sc = sb("dealt_sc", [P, H], U8)
         nc.vector.tensor_copy(dealt_sc[:].rearrange("p (t b i) -> p b t i", t=R, i=16), pick_sc[:].rearrange("p (b i t) -> p b t i", t=R, i=16))
         key_w = sb("key_w", [P, H], U32)
@@ -130,10 +130,8 @@ def tile_picked_pqkkindapagez_none_p_kernel(tc, x_words, x_scales, w1, tab, gs, 
             src = 16 * (j // 2) + j % 2
             nc.sync.dma_start(key_sc[j:P:32, :].bitcast(I32), dealt_sc[src:P:32, :].bitcast(I32))
 
-        gn16 = sb("gn16", [P, R], F32)
-        gn16n = sb("gn16n", [P, R], F32)
-        nc.scalar.activation(gn16[:], gn_sb[:], ACT.Copy, scale=0.0625)
-        nc.scalar.activation(gn16n[:], gn_sb[:], ACT.Copy, scale=-0.0625)
+        gn_neg = sb("gn_neg", [P, R], F32)
+        nc.scalar.activation(gn_neg[:], gn_sb[:], ACT.Copy, scale=-1.0)
 
         w2_bf = sb("w2_bf", [P, N, R], BF16)
         nc.scalar.copy(w2_bf[:].rearrange("p (c i) j -> p c j i", i=4), w2_raw[:].rearrange("p j (c i) -> p c j i", i=4))
@@ -141,14 +139,10 @@ def tile_picked_pqkkindapagez_none_p_kernel(tc, x_words, x_scales, w1, tab, gs, 
         score = [sb("score%d" % t, [P, 2 * S], F32) for t in range(R)]
         own = [sb("own%d" % t, [P, S], F32) for t in range(R)]
         s_bank = [psum.tile([P, S], F32, name="s_bank%d" % t, tag="b%d" % t) for t in range(R)]
-        pos = [sb("pos%d" % t, [P, S], F32) for t in range(R)]
 
-        def negative_part(t, cols):
-            nc.scalar.activation(pos[t][:, cols], s_bank[t][:, cols], ACT.Relu)
-            nc.scalar.activation(score[t][:, cols], pos[t][:, cols], ACT.Copy, scale=gn16n[:, t : t + 1])
-
-        def own_part(t, cols):
-            nc.scalar.activation(own[t][:, cols], s_bank[t][:, cols], ACT.Copy, scale=gn16[:, t : t + 1])
+        def leave_bank(t, cols):
+            nc.scalar.activation(score[t][:, cols], s_bank[t][:, cols], ACT.Relu, scale=0.0625)
+            nc.scalar.activation(own[t][:, cols], s_bank[t][:, cols], ACT.Copy, scale=0.0625)
 
         c0 = 0
         first = slice(0, Z_SLICES[0])
@@ -178,18 +172,13 @@ def tile_picked_pqkkindapagez_none_p_kernel(tc, x_words, x_scales, w1, tab, gs, 
                 kc = slice(P * t, P * t + P)
                 nc.tensor.matmul_mx(s_bank[t][:, cols], lhsT=key_w[:, kc].bitcast(FP8X4), lhsT_scale=key_sc[:, kc], rhs=z_w[:].bitcast(FP8X4), rhs_scale=z_sc[:], start=True, stop=True)
             if i == 0:
-                negative_part(0, first)
-                negative_part(1, first)
-                own_part(0, first)
-                own_part(1, first)
+                for t in range(R):
+                    leave_bank(t, first)
             c0 = c0 + width
-        nc.vector.tensor_scalar(score[0][:, rest], s_bank[0][:, rest], 0.0, gn16n[:, 0:1], ALU.max, ALU.mult)
-        own_part(0, rest)
-        negative_part(1, rest)
-        own_part(1, rest)
-        for t in range(2, R):
-            negative_part(t, slice(0, S))
-            own_part(t, slice(0, S))
+        nc.vector.tensor_scalar(score[0][:, rest], s_bank[0][:, rest], 0.0, 0.0625, ALU.max, ALU.mult)
+        nc.vector.tensor_scalar(own[0][:, rest], s_bank[0][:, rest], 0.0625, None, ALU.mult)
+        for t in range(1, R):
+            leave_bank(t, rest)
 
         def quantize_w2(m0, width, tag):
             words = sb("w2_w%d" % m0, [P, width], U32, tag=tag)
@@ -199,29 +188,33 @@ def tile_picked_pqkkindapagez_none_p_kernel(tc, x_words, x_scales, w1, tab, gs, 
 
         w2_q = quantize_w2(0, 2 * P, "z32_2")
 
-        z2_bf = [sb("z2_bf%d" % c, [P, width, R], BF16) for c, width in enumerate(OUT_CHUNKS)]
+        z2_bf = sb("z2_bf", [P, U, R], BF16)
 
-        def weave(t, c):
-            nc.scalar.copy(z2_bf[c][:, :, t], page[t][:, starts[c] : starts[c] + OUT_CHUNKS[c]])
+        def weave(t, cols):
+            nc.scalar.activation(z2_bf[:, cols, t], page[t][:, cols], ACT.Copy, scale=gn_neg[:, t : t + 1])
 
         fetched = [sb("fetched%d" % t, [P, S], F32) for t in range(R)]
 
         def fetch(t):
-            nc.vector.tensor_tensor(fetched[t][:], score[t][:].indirect(l_n5[:]), own[t][:], ALU.add)
+            nc.vector.tensor_tensor(fetched[t][:], score[t][:].indirect(l_n5[:]), own[t][:], ALU.subtract)
 
         def put(t):
             nc.vector.tensor_copy(page[t][:].indirect(l_n4[:]), fetched[t][:])
-            for c in range(len(OUT_CHUNKS)):
-                weave(t, c)
 
         fetch(0)
         fetch(1)
         put(0)
+        weave(0, slice(0, U))
+        fetch(2)
         put(1)
-        for t in range(2, R):
-            fetch(t)
-            w2_q.extend(quantize_w2(P * t, P, "pos%d" % t))
-            put(t)
+        weave(1, slice(0, U))
+        put(2)
+        weave(2, slice(0, U))
+        fetch(3)
+        w2_q.extend(quantize_w2(2 * P, 2 * P, "fetched2"))
+        put(3)
+        for c, width in enumerate(OUT_CHUNKS):
+            weave(3, slice(starts[c], starts[c] + width))
 
         z2_q = []
 
@@ -229,7 +222,7 @@ def tile_picked_pqkkindapagez_none_p_kernel(tc, x_words, x_scales, w1, tab, gs, 
             width = OUT_CHUNKS[c]
             words = sb("z2_w%d" % c, [P, width], U32, tag=("res%d_0" % (c - 2) if c >= 2 else None))
             scales = sb("z2_sc%d" % c, [P, width], U8)
-            nc.vector.quantize_mx(words[:].bitcast(FP8X4), scales[:], z2_bf[c][:].rearrange("p c j -> p (c j)"))
+            nc.vector.quantize_mx(words[:].bitcast(FP8X4), scales[:], z2_bf[:, starts[c] : starts[c] + width, :].rearrange("p c j -> p (c j)"))
             z2_q.append((words, scales))
 
         quantize_z2(0)
@@ -247,5 +240,7 @@ def tile_picked_pqkkindapagez_none_p_kernel(tc, x_words, x_scales, w1, tab, gs, 
                     ww, ws = w2_q[m]
                     nc.tensor.matmul_mx(bank[:, v, :], lhsT=ww.bitcast(FP8X4), lhsT_scale=ws, rhs=z2_q[c][0][:].bitcast(FP8X4), rhs_scale=z2_q[c][1][:], start=True, stop=True)
                 o_sb = sb("o_sb%d_%d" % (c, u), [P, per, width], F32)
-                nc.vector.tensor_tensor(o_sb[:], bank[:], res_sb[(c, u)][:], ALU.add)
-                nc.sync.dma_start(out_v[:, per * u : per * (u + 1), cols], o_sb[:])
+                pieces = [(0, 1), (1, 2)] if nb == 8 else [(0, per)]
+                for v0, v1 in pieces:
+                    nc.vector.tensor_tensor(o_sb[:, v0:v1, :], bank[:, v0:v1, :], res_sb[(c, u)][:, v0:v1, :], ALU.add)
+                    nc.sync.dma_start(out_v[:, per * u + v0 : per * u + v1, cols], o_sb[:, v0:v1, :])

@@ -14,10 +14,15 @@ ACT = mybir.ActivationFunctionType
 
 P = 128
 R = 4
+GROUP = 16
+BANK = 512
 K, T, S, N, H, J, G, U = 512, 1024, 512, 512, 512, 512, 2048, 1024
 FLOPS = 2 * K * H * S + 2 * K * H * S + 2 * H * N * U
+SCORE_SCALE = 0.0625
+
 Z_SLICES = (256, 128, 128)
 OUT_CHUNKS = (128, 128, 256, 256, 256)
+PAGES_ON_VECTOR = 2
 
 
 def tile_picked_pqkkindapagez_none_p_kernel(tc, x_words, x_scales, w1, tab, gs, d_words, d_scales, res, gn, w2, offs, n1, n2, n3, kidx, n4, n5, out):
@@ -30,9 +35,9 @@ def tile_picked_pqkkindapagez_none_p_kernel(tc, x_words, x_scales, w1, tab, gs, 
             return keep.tile(shape, dtype, name=name, tag=tag or name, align_bytes=64)
 
         def load_list(name, src):
-            t = keep.tile([P, S // 16], U16, name=name)
-            nc.sync.dma_start(t[:], src)
-            return t
+            offsets = keep.tile([P, S // GROUP], U16, name=name)
+            nc.sync.dma_start(offsets[:], src)
+            return offsets
 
         x_sc = sb("x_sc", [P, T], U8)
         d_sc = sb("d_sc", [P, G], U8)
@@ -41,11 +46,11 @@ def tile_picked_pqkkindapagez_none_p_kernel(tc, x_words, x_scales, w1, tab, gs, 
         nc.vector.memset(d_sc[:].bitcast(I32), 0)
         nc.vector.memset(key_sc[:].bitcast(I32), 0)
         page = [sb("page%d" % t, [P, U], F32) for t in range(R)]
-        for t in range(2):
+        for t in range(PAGES_ON_VECTOR):
             nc.vector.memset(page[t][:], 0.0)
         zero = sb("zero", [P, 8], F32)
         nc.gpsimd.memset(zero[:], 0.0)
-        for t in range(2, R):
+        for t in range(PAGES_ON_VECTOR, R):
             nc.scalar.copy(page[t][:], zero[:, 0:1].to_broadcast([P, U]))
 
         tab_v = tab.rearrange("(p t) c -> t p c", t=R)
@@ -63,14 +68,14 @@ def tile_picked_pqkkindapagez_none_p_kernel(tc, x_words, x_scales, w1, tab, gs, 
         xs_v = x_scales[0].bitcast(I32).rearrange("(q j) c -> j q c", j=4)
         for j in range(4):
             nc.sync.dma_start(x_sc[j:P:32, :].bitcast(I32), xs_v[j])
-        l_kidx = load_list("l_kidx", kidx)
-        d_w = sb("d_w", [P, G], U32)
-        nc.sync.dma_start(d_w[:].bitcast(I32), d_words[0].rearrange("p n r -> p (n r)").bitcast(I32))
         gs_sb = sb("gs_sb", [P, R], F32)
         nc.sync.dma_start(gs_sb[:], gs.rearrange("(p t) o -> p (t o)", t=R))
+        l_kidx = load_list("l_kidx", kidx)
         ds_v = d_scales[0].bitcast(I32).rearrange("(r e) c -> e r c", e=2)
         for e in range(2):
-            nc.sync.dma_start(d_sc[e:P:16, :].bitcast(I32), ds_v[e])
+            nc.sync.dma_start(d_sc[e:P:GROUP, :].bitcast(I32), ds_v[e])
+        d_w = sb("d_w", [P, G], U32)
+        nc.sync.dma_start(d_w[:].bitcast(I32), d_words[0].rearrange("p n r -> p (n r)").bitcast(I32))
         l_n3 = load_list("l_n3", n3)
         l_n2 = load_list("l_n2", n2)
         gn_sb = sb("gn_sb", [P, R], F32)
@@ -84,21 +89,21 @@ def tile_picked_pqkkindapagez_none_p_kernel(tc, x_words, x_scales, w1, tab, gs, 
         starts = [sum(OUT_CHUNKS[:c]) for c in range(len(OUT_CHUNKS))]
         res_sb = {}
         for c, width in enumerate(OUT_CHUNKS):
-            per = 512 // width
+            per = BANK // width
             for u in range(R // per):
                 res_sb[(c, u)] = sb("res%d_%d" % (c, u), [P, per, width], F32)
                 nc.sync.dma_start(res_sb[(c, u)][:], res_v[:, per * u : per * (u + 1), starts[c] : starts[c] + width])
 
         kind1 = [sb("kind1_%d" % t, [P, S], F32) for t in range(R)]
-        tabg = [sb("tabg%d" % t, [P, J], F32) for t in range(R)]
+        tab_gs = [sb("tab_gs%d" % t, [P, J], F32) for t in range(R)]
 
-        def gather_kinds(t):
+        def gather_n1(t):
             nc.vector.tensor_copy(kind1[t][:], tab_sb[t][:].indirect(l_n1[:]))
 
-        gather_kinds(0)
+        gather_n1(0)
         tok_w = sb("tok_w", [P, S], U32)
         nc.vector.tensor_copy(tok_w[:], x_w[:].indirect(l_offs[:]))
-        gather_kinds(1)
+        gather_n1(1)
         tok_sc = sb("tok_sc", [P, S], U8)
         nc.vector.tensor_copy(tok_sc[:], x_sc[:].indirect(l_offs[:]))
 
@@ -107,28 +112,28 @@ def tile_picked_pqkkindapagez_none_p_kernel(tc, x_words, x_scales, w1, tab, gs, 
         w1_w = sb("w1_w", [P, H], U32)
         w1_sc = sb("w1_sc", [P, H], U8)
         nc.vector.quantize_mx(w1_w[:].bitcast(FP8X4), w1_sc[:], w1_bf[:].rearrange("p t m j -> p (t m j)"))
-        gather_kinds(2)
-        gather_kinds(3)
+        gather_n1(2)
+        gather_n1(3)
 
-        y_sb = [sb("y%d" % t, [P, S], F32) for t in range(R)]
+        y_gs = [sb("y_gs%d" % t, [P, S], F32) for t in range(R)]
         for t in range(R):
             bank = psum.tile([P, S], F32, name="y_bank%d" % t, tag="a%d" % t)
             cols = slice(P * t, P * t + P)
             nc.tensor.matmul_mx(bank[:], lhsT=w1_w[:, cols].bitcast(FP8X4), lhsT_scale=w1_sc[:, cols], rhs=tok_w[:].bitcast(FP8X4), rhs_scale=tok_sc[:], start=True, stop=True)
-            nc.scalar.activation(y_sb[t][:, 0:S], bank[:], ACT.Copy, scale=gs_sb[:, t : t + 1])
-            nc.scalar.activation(tabg[t][:, 0:J], tab_sb[t][:, 0:J], ACT.Copy, scale=gs_sb[:, t : t + 1])
+            nc.scalar.activation(y_gs[t][:], bank[:], ACT.Copy, scale=gs_sb[:, t : t + 1])
+            nc.scalar.activation(tab_gs[t][:], tab_sb[t][:, 0:J], ACT.Copy, scale=gs_sb[:, t : t + 1])
 
-        pick_w = sb("pick_w", [P, H], U32)
-        nc.vector.tensor_copy(pick_w[:], d_w[:].indirect(l_kidx[:]))
         pick_sc = sb("pick_sc", [P, H], U8)
         nc.vector.tensor_copy(pick_sc[:], d_sc[:].indirect(l_kidx[:]))
+        pick_w = sb("pick_w", [P, H], U32)
+        nc.vector.tensor_copy(pick_w[:], d_w[:].indirect(l_kidx[:]))
         dealt_sc = sb("dealt_sc", [P, H], U8)
         nc.vector.tensor_copy(dealt_sc[:].rearrange("p (t b i) -> p b t i", t=R, i=16), pick_sc[:].rearrange("p (b i t) -> p b t i", t=R, i=16))
         key_w = sb("key_w", [P, H], U32)
         nc.vector.tensor_copy(key_w[:].rearrange("p (t b i) -> p b t i", t=R, i=4), pick_w[:].rearrange("p (b i t) -> p b t i", t=R, i=4))
         for j in range(4):
-            src = 16 * (j // 2) + j % 2
-            nc.sync.dma_start(key_sc[j:P:32, :].bitcast(I32), dealt_sc[src:P:32, :].bitcast(I32))
+            gathered_on = GROUP * (j // 2) + j % 2
+            nc.sync.dma_start(key_sc[j:P:32, :].bitcast(I32), dealt_sc[gathered_on:P:32, :].bitcast(I32))
 
         gn_neg = sb("gn_neg", [P, R], F32)
         nc.scalar.activation(gn_neg[:], gn_sb[:], ACT.Copy, scale=-1.0)
@@ -136,111 +141,106 @@ def tile_picked_pqkkindapagez_none_p_kernel(tc, x_words, x_scales, w1, tab, gs, 
         w2_bf = sb("w2_bf", [P, N, R], BF16)
         nc.scalar.copy(w2_bf[:].rearrange("p (c i) j -> p c j i", i=4), w2_raw[:].rearrange("p j (c i) -> p c j i", i=4))
 
-        score = [sb("score%d" % t, [P, 2 * S], F32) for t in range(R)]
-        own = [sb("own%d" % t, [P, S], F32) for t in range(R)]
+        s_pos = [sb("s_pos%d" % t, [P, 2 * S], F32) for t in range(R)]
+        s_own = [sb("s_own%d" % t, [P, S], F32) for t in range(R)]
         s_bank = [psum.tile([P, S], F32, name="s_bank%d" % t, tag="b%d" % t) for t in range(R)]
 
         def leave_bank(t, cols):
-            nc.scalar.activation(score[t][:, cols], s_bank[t][:, cols], ACT.Relu, scale=0.0625)
-            nc.scalar.activation(own[t][:, cols], s_bank[t][:, cols], ACT.Copy, scale=0.0625)
+            nc.scalar.activation(s_pos[t][:, cols], s_bank[t][:, cols], ACT.Relu, scale=SCORE_SCALE)
+            nc.scalar.activation(s_own[t][:, cols], s_bank[t][:, cols], ACT.Copy, scale=SCORE_SCALE)
 
-        c0 = 0
         first = slice(0, Z_SLICES[0])
         rest = slice(Z_SLICES[0], S)
+        last_slice = len(Z_SLICES) - 1
         for i, width in enumerate(Z_SLICES):
-            last = i == len(Z_SLICES) - 1
+            c0 = sum(Z_SLICES[:i])
             cols = slice(c0, c0 + width)
-            lcols = slice(c0 // 16, (c0 + width) // 16)
-            prod = sb("prod%d" % i, [P, R, width], F32, tag=("z_bf0" if last else None))
+            list_cols = slice(c0 // GROUP, (c0 + width) // GROUP)
+            prod = sb("prod%d" % i, [P, R, width], F32, tag=("z_bf0" if i == last_slice else None))
             z32 = sb("z32_%d" % i, [P, R, width], F32)
             for step in range(R + 1):
                 if step < R:
-                    nc.vector.tensor_tensor(prod[:, step, :], y_sb[step][:].indirect(l_n3[:, lcols]), kind1[step][:, cols], ALU.mult)
+                    nc.vector.tensor_tensor(prod[:, step, :], y_gs[step][:].indirect(l_n3[:, list_cols]), kind1[step][:, cols], ALU.mult)
                 if step > 0:
-                    nc.vector.tensor_tensor(z32[:, step - 1, :], tabg[step - 1][:].indirect(l_n2[:, lcols]), prod[:, step - 1, :], ALU.add)
+                    nc.vector.tensor_tensor(z32[:, step - 1, :], tab_gs[step - 1][:].indirect(l_n2[:, list_cols]), prod[:, step - 1, :], ALU.add)
             z_bf = sb("z_bf%d" % i, [P, width, R], BF16)
-            dst = z_bf[:].rearrange("p (c i) j -> p c j i", i=4)
-            srcv = z32[:].rearrange("p j (c i) -> p c j i", i=4)
-            if last:
-                nc.vector.tensor_copy(dst, srcv)
+            side_by_side = z_bf[:].rearrange("p (c i) j -> p c j i", i=4)
+            planes = z32[:].rearrange("p j (c i) -> p c j i", i=4)
+            if i == last_slice:
+                nc.vector.tensor_copy(side_by_side, planes)
             else:
-                nc.scalar.copy(dst, srcv)
+                nc.scalar.copy(side_by_side, planes)
             z_w = sb("z_w%d" % i, [P, width], U32)
             z_sc = sb("z_sc%d" % i, [P, width], U8)
             nc.vector.quantize_mx(z_w[:].bitcast(FP8X4), z_sc[:], z_bf[:].rearrange("p c j -> p (c j)"))
             for t in range(R):
-                kc = slice(P * t, P * t + P)
-                nc.tensor.matmul_mx(s_bank[t][:, cols], lhsT=key_w[:, kc].bitcast(FP8X4), lhsT_scale=key_sc[:, kc], rhs=z_w[:].bitcast(FP8X4), rhs_scale=z_sc[:], start=True, stop=True)
+                keys = slice(P * t, P * t + P)
+                nc.tensor.matmul_mx(s_bank[t][:, cols], lhsT=key_w[:, keys].bitcast(FP8X4), lhsT_scale=key_sc[:, keys], rhs=z_w[:].bitcast(FP8X4), rhs_scale=z_sc[:], start=True, stop=True)
             if i == 0:
                 for t in range(R):
                     leave_bank(t, first)
-            c0 = c0 + width
-        nc.vector.tensor_scalar(score[0][:, rest], s_bank[0][:, rest], 0.0, 0.0625, ALU.max, ALU.mult)
-        nc.vector.tensor_scalar(own[0][:, rest], s_bank[0][:, rest], 0.0625, None, ALU.mult)
+        nc.vector.tensor_scalar(s_pos[0][:, rest], s_bank[0][:, rest], 0.0, SCORE_SCALE, ALU.max, ALU.mult)
+        nc.vector.tensor_scalar(s_own[0][:, rest], s_bank[0][:, rest], SCORE_SCALE, None, ALU.mult)
         for t in range(1, R):
             leave_bank(t, rest)
 
-        def quantize_w2(m0, width, tag):
-            words = sb("w2_w%d" % m0, [P, width], U32, tag=tag)
-            scales = sb("w2_sc%d" % m0, [P, width], U8)
-            nc.vector.quantize_mx(words[:].bitcast(FP8X4), scales[:], w2_bf[:, m0 : m0 + width, :].rearrange("p c j -> p (c j)"))
-            return [(words[:, b : b + P], scales[:, b : b + P]) for b in range(0, width, P)]
+        def quantize_w2(m0, after):
+            words = sb("w2_w%d" % m0, [P, N // 2], U32, tag=after)
+            scales = sb("w2_sc%d" % m0, [P, N // 2], U8)
+            nc.vector.quantize_mx(words[:].bitcast(FP8X4), scales[:], w2_bf[:, m0 : m0 + N // 2, :].rearrange("p c j -> p (c j)"))
+            return [(words[:, b : b + P], scales[:, b : b + P]) for b in range(0, N // 2, P)]
 
-        w2_q = quantize_w2(0, 2 * P, "z32_2")
+        w2_q = quantize_w2(0, "z32_%d" % last_slice)
 
         z2_bf = sb("z2_bf", [P, U, R], BF16)
+        nw_neg = [sb("nw_neg%d" % t, [P, S], F32) for t in range(R)]
+
+        def fetch(t):
+            nc.vector.tensor_tensor(nw_neg[t][:], s_pos[t][:].indirect(l_n5[:]), s_own[t][:], ALU.subtract)
+
+        def put(t):
+            nc.vector.tensor_copy(page[t][:].indirect(l_n4[:]), nw_neg[t][:])
 
         def weave(t, cols):
             nc.scalar.activation(z2_bf[:, cols, t], page[t][:, cols], ACT.Copy, scale=gn_neg[:, t : t + 1])
 
-        fetched = [sb("fetched%d" % t, [P, S], F32) for t in range(R)]
-
-        def fetch(t):
-            nc.vector.tensor_tensor(fetched[t][:], score[t][:].indirect(l_n5[:]), own[t][:], ALU.subtract)
-
-        def put(t):
-            nc.vector.tensor_copy(page[t][:].indirect(l_n4[:]), fetched[t][:])
-
+        chunks = [slice(starts[c], starts[c] + width) for c, width in enumerate(OUT_CHUNKS)]
         fetch(0)
-        fetch(1)
-        put(0)
-        weave(0, slice(0, U))
-        fetch(2)
-        put(1)
-        weave(1, slice(0, U))
-        put(2)
-        weave(2, slice(0, U))
-        fetch(3)
-        w2_q.extend(quantize_w2(2 * P, 2 * P, "fetched2"))
-        put(3)
-        for c, width in enumerate(OUT_CHUNKS):
-            weave(3, slice(starts[c], starts[c] + width))
+        for t in range(R - 1):
+            fetch(t + 1)
+            put(t)
+            weave(t, slice(0, U if t < R - 2 else chunks[-1].start))
+        put(R - 1)
+        w2_q.extend(quantize_w2(N // 2, "nw_neg%d" % (R - 1)))
+        for cols in chunks[:-2]:
+            weave(R - 1, cols)
+        weave(R - 2, chunks[-1])
+        for cols in chunks[-2:]:
+            weave(R - 1, cols)
 
         z2_q = []
 
         def quantize_z2(c):
-            width = OUT_CHUNKS[c]
-            words = sb("z2_w%d" % c, [P, width], U32, tag=("res%d_0" % (c - 2) if c >= 2 else None))
-            scales = sb("z2_sc%d" % c, [P, width], U8)
-            nc.vector.quantize_mx(words[:].bitcast(FP8X4), scales[:], z2_bf[:, starts[c] : starts[c] + width, :].rearrange("p c j -> p (c j)"))
+            words = sb("z2_w%d" % c, [P, OUT_CHUNKS[c]], U32, tag=("res%d_0" % (c - 2) if c >= 2 else None))
+            scales = sb("z2_sc%d" % c, [P, OUT_CHUNKS[c]], U8)
+            nc.vector.quantize_mx(words[:].bitcast(FP8X4), scales[:], z2_bf[:, chunks[c], :].rearrange("p c j -> p (c j)"))
             z2_q.append((words, scales))
 
+        bank_tags = ["a%d" % t for t in range(R)] + ["b%d" % t for t in range(R)]
+        banks_used = 0
         quantize_z2(0)
-        nb = 0
         for c, width in enumerate(OUT_CHUNKS):
             if c + 1 < len(OUT_CHUNKS):
                 quantize_z2(c + 1)
-            cols = slice(starts[c], starts[c] + width)
-            per = 512 // width
+            per = BANK // width
             for u in range(R // per):
-                bank = psum.tile([P, per, width], F32, name="o_bank%d_%d" % (c, u), tag="%s%d" % ("ab"[nb // 4], nb % 4))
-                nb = nb + 1
+                bank = psum.tile([P, per, width], F32, name="o_bank%d_%d" % (c, u), tag=bank_tags[banks_used])
+                banks_used = banks_used + 1
                 for v in range(per):
-                    m = per * u + v
-                    ww, ws = w2_q[m]
-                    nc.tensor.matmul_mx(bank[:, v, :], lhsT=ww.bitcast(FP8X4), lhsT_scale=ws, rhs=z2_q[c][0][:].bitcast(FP8X4), rhs_scale=z2_q[c][1][:], start=True, stop=True)
+                    words, scales = w2_q[per * u + v]
+                    nc.tensor.matmul_mx(bank[:, v, :], lhsT=words.bitcast(FP8X4), lhsT_scale=scales, rhs=z2_q[c][0][:].bitcast(FP8X4), rhs_scale=z2_q[c][1][:], start=True, stop=True)
                 o_sb = sb("o_sb%d_%d" % (c, u), [P, per, width], F32)
-                pieces = [(0, 1), (1, 2)] if nb == 8 else [(0, per)]
-                for v0, v1 in pieces:
-                    nc.vector.tensor_tensor(o_sb[:, v0:v1, :], bank[:, v0:v1, :], res_sb[(c, u)][:, v0:v1, :], ALU.add)
-                    nc.sync.dma_start(out_v[:, per * u + v0 : per * u + v1, cols], o_sb[:, v0:v1, :])
+                blocks = per if banks_used < len(bank_tags) else 1
+                for v in range(0, per, blocks):
+                    nc.vector.tensor_tensor(o_sb[:, v : v + blocks, :], bank[:, v : v + blocks, :], res_sb[(c, u)][:, v : v + blocks, :], ALU.add)
+                    nc.sync.dma_start(out_v[:, per * u + v : per * u + v + blocks, chunks[c]], o_sb[:, v : v + blocks, :])

from contextlib import ExitStack

import concourse.mybir as mybir

F32 = mybir.dt.float32
BF16 = mybir.dt.bfloat16
I32 = mybir.dt.int32
U32 = mybir.dt.uint32
U16 = mybir.dt.uint16
U8 = mybir.dt.uint8
FP8X4 = mybir.dt.float8_e4m3fn_x4
ALU = mybir.AluOpType
ACT = mybir.ActivationFunctionType

P = 128
R = 4
GROUP = 16
BANK = 512
K, T, S, N, H, J, G, U = 512, 1024, 512, 512, 512, 512, 2048, 1024
FLOPS = 2 * K * H * S + 2 * K * H * S + 2 * H * N * U
SCORE_SCALE = 0.0625

Z_SLICES = (256, 128, 128)
OUT_CHUNKS = (128, 128, 256, 256, 256)
PAGES_ON_VECTOR = 2


def tile_picked_pqkkindapagez_none_p_kernel(tc, x_words, x_scales, w1, tab, gs, d_words, d_scales, res, gn, w2, offs, n1, n2, n3, kidx, n4, n5, out):
    nc = tc.nc
    with ExitStack() as ctx:
        keep = ctx.enter_context(tc.tile_pool(name="keep", bufs=1))
        psum = ctx.enter_context(tc.psum_pool(name="psum", bufs=1))

        def sb(name, shape, dtype, tag=None):
            return keep.tile(shape, dtype, name=name, tag=tag or name, align_bytes=64)

        def load_list(name, src):
            offsets = keep.tile([P, S // GROUP], U16, name=name)
            nc.sync.dma_start(offsets[:], src)
            return offsets

        x_sc = sb("x_sc", [P, T], U8)
        d_sc = sb("d_sc", [P, G], U8)
        key_sc = sb("key_sc", [P, H], U8)
        nc.vector.memset(x_sc[:].bitcast(I32), 0)
        nc.vector.memset(d_sc[:].bitcast(I32), 0)
        nc.vector.memset(key_sc[:].bitcast(I32), 0)
        page = [sb("page%d" % t, [P, U], F32) for t in range(R)]
        for t in range(PAGES_ON_VECTOR):
            nc.vector.memset(page[t][:], 0.0)
        zero = sb("zero", [P, 8], F32)
        nc.gpsimd.memset(zero[:], 0.0)
        for t in range(PAGES_ON_VECTOR, R):
            nc.scalar.copy(page[t][:], zero[:, 0:1].to_broadcast([P, U]))

        tab_v = tab.rearrange("(p t) c -> t p c", t=R)
        tab_sb = [sb("tab%d" % t, [P, 2 * J], F32) for t in range(R)]
        nc.sync.dma_start(tab_sb[0][:, 0:J], tab_v[0])
        l_n1 = load_list("l_n1", n1)
        l_offs = load_list("l_offs", offs)
        x_w = sb("x_w", [P, T], U32)
        nc.sync.dma_start(x_w[:].bitcast(I32), x_words[0].rearrange("p n r -> p (n r)").bitcast(I32))
        nc.sync.dma_start(tab_sb[1][:, 0:J], tab_v[1])
        w1_raw = sb("w1_raw", [P, R, H], F32)
        nc.sync.dma_start(w1_raw[:], w1.rearrange("(p j) c -> p j c", j=R))
        nc.sync.dma_start(tab_sb[2][:, 0:J], tab_v[2])
        nc.sync.dma_start(tab_sb[3][:, 0:J], tab_v[3])
        xs_v = x_scales[0].bitcast(I32).rearrange("(q j) c -> j q c", j=4)
        for j in range(4):
            nc.sync.dma_start(x_sc[j:P:32, :].bitcast(I32), xs_v[j])
        gs_sb = sb("gs_sb", [P, R], F32)
        nc.sync.dma_start(gs_sb[:], gs.rearrange("(p t) o -> p (t o)", t=R))
        l_kidx = load_list("l_kidx", kidx)
        ds_v = d_scales[0].bitcast(I32).rearrange("(r e) c -> e r c", e=2)
        for e in range(2):
            nc.sync.dma_start(d_sc[e:P:GROUP, :].bitcast(I32), ds_v[e])
        d_w = sb("d_w", [P, G], U32)
        nc.sync.dma_start(d_w[:].bitcast(I32), d_words[0].rearrange("p n r -> p (n r)").bitcast(I32))
        l_n3 = load_list("l_n3", n3)
        l_n2 = load_list("l_n2", n2)
        gn_sb = sb("gn_sb", [P, R], F32)
        nc.sync.dma_start(gn_sb[:], gn.rearrange("(p t) o -> p (t o)", t=R))
        w2_raw = sb("w2_raw", [P, R, N], F32)
        nc.sync.dma_start(w2_raw[:], w2.rearrange("(p j) c -> p j c", j=R))
        l_n5 = load_list("l_n5", n5)
        l_n4 = load_list("l_n4", n4)
        res_v = res.rearrange("(t p) w -> p t w", p=P)
        out_v = out.rearrange("(t p) w -> p t w", p=P)
        starts = [sum(OUT_CHUNKS[:c]) for c in range(len(OUT_CHUNKS))]
        res_sb = {}
        for c, width in enumerate(OUT_CHUNKS):
            per = BANK // width
            for u in range(R // per):
                res_sb[(c, u)] = sb("res%d_%d" % (c, u), [P, per, width], F32)
                nc.sync.dma_start(res_sb[(c, u)][:], res_v[:, per * u : per * (u + 1), starts[c] : starts[c] + width])

        kind1 = [sb("kind1_%d" % t, [P, S], F32) for t in range(R)]
        tab_gs = [sb("tab_gs%d" % t, [P, J], F32) for t in range(R)]

        def gather_n1(t):
            nc.vector.tensor_copy(kind1[t][:], tab_sb[t][:].indirect(l_n1[:]))

        gather_n1(0)
        tok_w = sb("tok_w", [P, S], U32)
        nc.vector.tensor_copy(tok_w[:], x_w[:].indirect(l_offs[:]))
        gather_n1(1)
        tok_sc = sb("tok_sc", [P, S], U8)
        nc.vector.tensor_copy(tok_sc[:], x_sc[:].indirect(l_offs[:]))

        w1_bf = sb("w1_bf", [P, R, P, R], BF16)
        nc.scalar.copy(w1_bf[:].rearrange("p t m j -> p m t j"), w1_raw[:].rearrange("p j (m t) -> p m t j", t=R))
        w1_w = sb("w1_w", [P, H], U32)
        w1_sc = sb("w1_sc", [P, H], U8)
        nc.vector.quantize_mx(w1_w[:].bitcast(FP8X4), w1_sc[:], w1_bf[:].rearrange("p t m j -> p (t m j)"))
        gather_n1(2)
        gather_n1(3)

        y_gs = [sb("y_gs%d" % t, [P, S], F32) for t in range(R)]
        for t in range(R):
            bank = psum.tile([P, S], F32, name="y_bank%d" % t, tag="a%d" % t)
            cols = slice(P * t, P * t + P)
            nc.tensor.matmul_mx(bank[:], lhsT=w1_w[:, cols].bitcast(FP8X4), lhsT_scale=w1_sc[:, cols], rhs=tok_w[:].bitcast(FP8X4), rhs_scale=tok_sc[:], start=True, stop=True)
            nc.scalar.activation(y_gs[t][:], bank[:], ACT.Copy, scale=gs_sb[:, t : t + 1])
            nc.scalar.activation(tab_gs[t][:], tab_sb[t][:, 0:J], ACT.Copy, scale=gs_sb[:, t : t + 1])

        pick_sc = sb("pick_sc", [P, H], U8)
        nc.vector.tensor_copy(pick_sc[:], d_sc[:].indirect(l_kidx[:]))
        pick_w = sb("pick_w", [P, H], U32)
        nc.vector.tensor_copy(pick_w[:], d_w[:].indirect(l_kidx[:]))
        dealt_sc = sb("dealt_sc", [P, H], U8)
        nc.vector.tensor_copy(dealt_sc[:].rearrange("p (t b i) -> p b t i", t=R, i=16), pick_sc[:].rearrange("p (b i t) -> p b t i", t=R, i=16))
        key_w = sb("key_w", [P, H], U32)
        nc.vector.tensor_copy(key_w[:].rearrange("p (t b i) -> p b t i", t=R, i=4), pick_w[:].rearrange("p (b i t) -> p b t i", t=R, i=4))
        for j in range(4):
            gathered_on = GROUP * (j // 2) + j % 2
            nc.sync.dma_start(key_sc[j:P:32, :].bitcast(I32), dealt_sc[gathered_on:P:32, :].bitcast(I32))

        gn_neg = sb("gn_neg", [P, R], F32)
        nc.scalar.activation(gn_neg[:], gn_sb[:], ACT.Copy, scale=-1.0)

        w2_bf = sb("w2_bf", [P, N, R], BF16)
        nc.scalar.copy(w2_bf[:].rearrange("p (c i) j -> p c j i", i=4), w2_raw[:].rearrange("p j (c i) -> p c j i", i=4))

        s_pos = [sb("s_pos%d" % t, [P, 2 * S], F32) for t in range(R)]
        s_own = [sb("s_own%d" % t, [P, S], F32) for t in range(R)]
        s_bank = [psum.tile([P, S], F32, name="s_bank%d" % t, tag="b%d" % t) for t in range(R)]

        def leave_bank(t, cols):
            nc.scalar.activation(s_pos[t][:, cols], s_bank[t][:, cols], ACT.Relu, scale=SCORE_SCALE)
            nc.scalar.activation(s_own[t][:, cols], s_bank[t][:, cols], ACT.Copy, scale=SCORE_SCALE)

        first = slice(0, Z_SLICES[0])
        rest = slice(Z_SLICES[0], S)
        last_slice = len(Z_SLICES) - 1
        for i, width in enumerate(Z_SLICES):
            c0 = sum(Z_SLICES[:i])
            cols = slice(c0, c0 + width)
            list_cols = slice(c0 // GROUP, (c0 + width) // GROUP)
            prod = sb("prod%d" % i, [P, R, width], F32, tag=("z_bf0" if i == last_slice else None))
            z32 = sb("z32_%d" % i, [P, R, width], F32)
            for step in range(R + 1):
                if step < R:
                    nc.vector.tensor_tensor(prod[:, step, :], y_gs[step][:].indirect(l_n3[:, list_cols]), kind1[step][:, cols], ALU.mult)
                if step > 0:
                    nc.vector.tensor_tensor(z32[:, step - 1, :], tab_gs[step - 1][:].indirect(l_n2[:, list_cols]), prod[:, step - 1, :], ALU.add)
            z_bf = sb("z_bf%d" % i, [P, width, R], BF16)
            side_by_side = z_bf[:].rearrange("p (c i) j -> p c j i", i=4)
            planes = z32[:].rearrange("p j (c i) -> p c j i", i=4)
            if i == last_slice:
                nc.vector.tensor_copy(side_by_side, planes)
            else:
                nc.scalar.copy(side_by_side, planes)
            z_w = sb("z_w%d" % i, [P, width], U32)
            z_sc = sb("z_sc%d" % i, [P, width], U8)
            nc.vector.quantize_mx(z_w[:].bitcast(FP8X4), z_sc[:], z_bf[:].rearrange("p c j -> p (c j)"))
            for t in range(R):
                keys = slice(P * t, P * t + P)
                nc.tensor.matmul_mx(s_bank[t][:, cols], lhsT=key_w[:, keys].bitcast(FP8X4), lhsT_scale=key_sc[:, keys], rhs=z_w[:].bitcast(FP8X4), rhs_scale=z_sc[:], start=True, stop=True)
            if i == 0:
                for t in range(R):
                    leave_bank(t, first)
        nc.vector.tensor_scalar(s_pos[0][:, rest], s_bank[0][:, rest], 0.0, SCORE_SCALE, ALU.max, ALU.mult)
        nc.vector.tensor_scalar(s_own[0][:, rest], s_bank[0][:, rest], SCORE_SCALE, None, ALU.mult)
        for t in range(1, R):
            leave_bank(t, rest)

        def quantize_w2(m0, after):
            words = sb("w2_w%d" % m0, [P, N // 2], U32, tag=after)
            scales = sb("w2_sc%d" % m0, [P, N // 2], U8)
            nc.vector.quantize_mx(words[:].bitcast(FP8X4), scales[:], w2_bf[:, m0 : m0 + N // 2, :].rearrange("p c j -> p (c j)"))
            return [(words[:, b : b + P], scales[:, b : b + P]) for b in range(0, N // 2, P)]

        w2_q = quantize_w2(0, "z32_%d" % last_slice)

        z2_bf = sb("z2_bf", [P, U, R], BF16)
        nw_neg = [sb("nw_neg%d" % t, [P, S], F32) for t in range(R)]

        def fetch(t):
            nc.vector.tensor_tensor(nw_neg[t][:], s_pos[t][:].indirect(l_n5[:]), s_own[t][:], ALU.subtract)

        def put(t):
            nc.vector.tensor_copy(page[t][:].indirect(l_n4[:]), nw_neg[t][:])

        def weave(t, cols):
            nc.scalar.activation(z2_bf[:, cols, t], page[t][:, cols], ACT.Copy, scale=gn_neg[:, t : t + 1])

        chunks = [slice(starts[c], starts[c] + width) for c, width in enumerate(OUT_CHUNKS)]
        fetch(0)
        for t in range(R - 1):
            fetch(t + 1)
            put(t)
            weave(t, slice(0, U if t < R - 2 else chunks[-1].start))
        put(R - 1)
        w2_q.extend(quantize_w2(N // 2, "nw_neg%d" % (R - 1)))
        for cols in chunks[:-2]:
            weave(R - 1, cols)
        weave(R - 2, chunks[-1])
        for cols in chunks[-2:]:
            weave(R - 1, cols)

        z2_q = []

        def quantize_z2(c):
            words = sb("z2_w%d" % c, [P, OUT_CHUNKS[c]], U32, tag=("res%d_0" % (c - 2) if c >= 2 else None))
            scales = sb("z2_sc%d" % c, [P, OUT_CHUNKS[c]], U8)
            nc.vector.quantize_mx(words[:].bitcast(FP8X4), scales[:], z2_bf[:, chunks[c], :].rearrange("p c j -> p (c j)"))
            z2_q.append((words, scales))

        bank_tags = ["a%d" % t for t in range(R)] + ["b%d" % t for t in range(R)]
        banks_used = 0
        quantize_z2(0)
        for c, width in enumerate(OUT_CHUNKS):
            if c + 1 < len(OUT_CHUNKS):
                quantize_z2(c + 1)
            per = BANK // width
            for u in range(R // per):
                bank = psum.tile([P, per, width], F32, name="o_bank%d_%d" % (c, u), tag=bank_tags[banks_used])
                banks_used = banks_used + 1
                for v in range(per):
                    words, scales = w2_q[per * u + v]
                    nc.tensor.matmul_mx(bank[:, v, :], lhsT=words.bitcast(FP8X4), lhsT_scale=scales, rhs=z2_q[c][0][:].bitcast(FP8X4), rhs_scale=z2_q[c][1][:], start=True, stop=True)
                o_sb = sb("o_sb%d_%d" % (c, u), [P, per, width], F32)
                blocks = per if banks_used < len(bank_tags) else 1
                for v in range(0, per, blocks):
                    nc.vector.tensor_tensor(o_sb[:, v : v + blocks, :], bank[:, v : v + blocks, :], res_sb[(c, u)][:, v : v + blocks, :], ALU.add)
                    nc.sync.dma_start(out_v[:, per * u + v : per * u + v + blocks, chunks[c]], o_sb[:, v : v + blocks, :])
